import numpy as np
import ml_dtypes


def mxq(x, axis, fmt="e4m3"):
    dtype, down = {"e4m3": (ml_dtypes.float8_e4m3fn, 7), "e5m2": (ml_dtypes.float8_e5m2, 14)}[fmt]
    v = np.moveaxis(np.asarray(x, np.float32).astype(ml_dtypes.bfloat16).astype(np.float64), axis, -1)
    blocks = v.reshape(v.shape[:-1] + (-1, 32))
    amax = np.abs(blocks).max(-1, keepdims=True)
    byte = np.maximum(np.where(amax > 0, np.frexp(amax)[1] - 1 + 127, 0) - down, 1)
    scale = np.exp2(byte - 127.0)
    codes = (blocks / scale).astype(np.float32).astype(dtype).astype(np.float64)
    return np.moveaxis((codes * scale).reshape(v.shape), -1, axis)


WIDE = False


def mx_kscale(k):
    if not WIDE:
        return np.ones(k)
    levels = np.array([10, -10, 5, -5, 0])
    if k % 512:
        return np.exp2(np.random.permutation(np.resize(levels, k // 32))).repeat(32)
    a = np.empty((k // 512, 16))
    for p in range(k // 512):
        a[p, :8] = np.random.permutation(np.resize(levels, 8))
        for g in range(8):
            far = levels[np.abs(levels - a[p, g]) >= 10]
            a[p, g + 8] = far[np.random.randint(len(far))]
    return np.exp2(a.ravel()).repeat(32)


BF16 = ml_dtypes.bfloat16


def bf(x):
    return np.asarray(x, np.float32).astype(BF16)


def f64(x):
    return np.asarray(x).astype(np.float64)


E2M1 = np.array([0.0, 0.5, 1.0, 1.5, 2.0, 3.0, 4.0, 6.0, -0.0, -0.5, -1.0, -1.5, -2.0, -3.0, -4.0, -6.0])


def pack_weight(w, fmt):
    k, n = w.shape
    w = f64(bf(w)).reshape(k // 32, 32, n)
    amax = np.abs(w).max(1)
    if fmt == "e4m3":
        byte = np.frexp(amax)[1] - 1 + 127 - 7
    else:
        mant, ex = np.frexp(amax / 6.0)
        byte = np.where(mant > 0.5, ex, ex - 1) + 127
    byte = np.clip(np.where(amax > 0, byte, 1), 1, 254)
    scaled = (w * np.exp2(127.0 - byte)[:, None, :]).reshape(k, n).astype(np.float32)
    by_word = np.ascontiguousarray(scaled.reshape(k // 512, 128, 4, n).transpose(0, 1, 3, 2))
    if fmt == "e4m3":
        words = by_word.astype(ml_dtypes.float8_e4m3fn).view(np.uint8)
    else:
        c = by_word.astype(ml_dtypes.float4_e2m1fn).view(np.uint8) & 0xF
        words = c[..., 0::2] | (c[..., 1::2] << 4)
    return np.ascontiguousarray(words), np.ascontiguousarray(byte.astype(np.uint8).reshape(k // 512, 16, n))


def unpack_weight(words, scales, fmt):
    g, p, n, _ = words.shape
    if fmt == "e4m3":
        vals = np.ascontiguousarray(words).view(ml_dtypes.float8_e4m3fn).astype(np.float64)
    else:
        nib = np.empty((g, p, n, 4), np.uint8)
        nib[..., 0::2] = words & 0xF
        nib[..., 1::2] = words >> 4
        vals = E2M1[nib]
    vals = vals * np.repeat(np.exp2(scales.astype(np.float64) - 127.0), 8, axis=1)[..., None]
    return vals.transpose(0, 1, 3, 2).reshape(g * 512, n)
def pack4(w):
    words, scales = pack_weight(w, "e2m1")
    return words.reshape(words.shape[0], 128, -1), scales


def unpack4(words, scales):
    return unpack_weight(words.reshape(words.shape[0], 128, -1, 2), scales, "e2m1")


def planes(Y):
    n, m = Y.shape
    b = f64(bf(Y)).reshape(n // 32, 32, m)
    amax = np.abs(b).max(1)
    byte = np.clip(np.where(amax > 0, np.frexp(amax)[1] - 1 + 127 - 7, 1), 1, 254)
    codes = (b * np.exp2(127.0 - byte)[:, None, :]).reshape(n, m).astype(np.float32).astype(ml_dtypes.float8_e4m3fn).view(np.uint8)
    words = codes.reshape(n // 512, 128, 4, m).transpose(0, 1, 3, 2)
    return np.ascontiguousarray(words), np.ascontiguousarray(byte.astype(np.uint8).reshape(n // 512, 16, m))


S, M = 2048, 1024
CENTS = 50.0
TABLE_SPREAD = 1.2
INTENSITY_SPREAD = 0.8


def setup_inputs():
    s = mx_kscale(S)
    x = np.random.randn(S, M) * s[:, None]
    x_words, x_scales = pack_weight(x, "e4m3")
    table = np.exp(TABLE_SPREAD * np.random.randn(S, S) - TABLE_SPREAD ** 2 / 2)
    a = table * (CENTS / S) / s[None, :]
    d = np.random.randn(S, M)
    e = 0.5 * np.exp(INTENSITY_SPREAD * np.random.randn(S))
    return {"x_words": x_words, "x_scales": x_scales,
            "a": bf(a), "d": bf(d), "e": bf(e)}


def reference(x_words, x_scales, a, d, e):
    x = unpack_weight(x_words, x_scales, "e4m3")
    inter = mxq(f64(a), 1, "e4m3") @ x
    total = inter + f64(d)
    y = f64(e)[:, None] * total
    Y = y
    words, scales = planes(Y)
    return y, words, scales

@@ -1,0 +1,264 @@
+from contextlib import ExitStack
+
+import concourse.mybir as mybir
+from concourse.masks import make_identity
+
+S, M = 2048, 1024
+FLOPS = 2 * S * S * M
+
+F32 = mybir.dt.float32
+BF16 = mybir.dt.bfloat16
+I32 = mybir.dt.int32
+U8 = mybir.dt.uint8
+FP8X4 = mybir.dt.float8_e4m3fn_x4
+ALU = mybir.AluOpType
+ACT = mybir.ActivationFunctionType
+
+P = 128
+PACK = 4
+K_PASS = P * PACK
+PASSES = S // K_PASS
+BANK = 512
+ROW_TILES = S // P
+
+SORT_FROM = 16
+SORT_V = 4
+RUN = 1
+ED_AHEAD = 6
+ILV_S = [0,0,0,0,0,0,6,8,3,3]
+LOADS_FIRST = 21
+LOADS_PER_STORE = 3
+
+
+def tile_sector_emission_changes_g6_kernel(tc, x_words, x_scales, a, d, e, out_0, out_1, out_2):
+    nc = tc.nc
+    units = [(0, 0, 512), (1, 0, 512), (0, 512, 512), (1, 512, 512), (2, 0, 512), (2, 512, 512), (3, 0, 512), (3, 512, 256), (3, 768, 256)]
+    groups = [(u, t) for u in range(len(units)) for t in range(PACK)]
+
+    with ExitStack() as ctx:
+        keep = ctx.enter_context(tc.tile_pool(name="keep", bufs=1))
+        work = ctx.enter_context(tc.tile_pool(name="work", bufs=2))
+        psum = ctx.enter_context(tc.psum_pool(name="psum", bufs=4))
+
+        ident = keep.tile([P, P], F32, name="ident")
+        make_identity(nc, ident[:])
+        ctx.enter_context(tc.manual_schedule())
+
+        x_plane = keep.tile([P, M], U8, name="x_plane", align_bytes=64)
+        y_plane = keep.tile([P, M], U8, name="y_plane", align_bytes=64)
+        e_bf = keep.tile([P, PASSES, PACK], BF16, name="e_bf")
+        e_f32 = keep.tile([P, PASSES, PACK], F32, name="e_f32")
+        nc.vector.memset(x_plane[:].bitcast(I32), 0)
+
+        a_words = {}
+        a_full = {}
+        x_codes = {}
+        d_rows = {}
+
+        def load_a(j0, count, kg0, kg1):
+            g, t0 = divmod(j0, PACK)
+            tile = keep.tile([P, count, (kg1 - kg0) * K_PASS], BF16, name="a_%d_%d" % (j0, kg0), align_bytes=64)
+            rows = a[g * K_PASS:(g + 1) * K_PASS, kg0 * K_PASS:kg1 * K_PASS].rearrange("(m t) k -> m t k", t=PACK)
+            nc.sync.dma_start(out=tile[:], in_=rows[:, t0:t0 + count, :])
+            for n in range(count):
+                words = tile[:, n, :].bitcast(F32)
+                a_full[j0 + n] = words
+                for kg in range(kg0, kg1):
+                    a_words[(j0 + n, kg)] = words[:, (kg - kg0) * 2 * P:(kg - kg0 + 1) * 2 * P]
+
+        def load_x(h, kg0, kg1):
+            tile = keep.tile([P, kg1 - kg0, BANK], I32, name="x_%d_%d" % (h, kg0), align_bytes=64)
+            src = x_words[kg0:kg1, :, h * BANK:(h + 1) * BANK, :].rearrange("g p n t -> p g (n t)")
+            nc.sync.dma_start(out=tile[:], in_=src.bitcast(I32))
+            for kg in range(kg0, kg1):
+                x_codes[(kg, h)] = tile[:, kg - kg0, :]
+
+        def load_d(g, h0, h1):
+            tile = keep.tile([P, PACK, (h1 - h0) * BANK], BF16, name="d_%d_%d" % (g, h0))
+            src = d[g * K_PASS:(g + 1) * K_PASS, h0 * BANK:h1 * BANK].rearrange("(p t) c -> p t c", t=PACK)
+            nc.sync.dma_start(out=tile[:], in_=src)
+            for h in range(h0, h1):
+                d_rows[(g, h)] = tile[:, :, (h - h0) * BANK:(h - h0 + 1) * BANK]
+
+        def load_small():
+            for q in range(4):
+                nc.scalar.dma_start(out=x_plane[32 * q:32 * q + 16, :].bitcast(I32),
+                                    in_=x_scales[:, 4 * q:4 * q + 4, :].bitcast(I32))
+
+        def load_e():
+            nc.scalar.dma_start(out=e_bf[:], in_=e.rearrange("(g p t) -> p g t", p=P, t=PACK))
+
+        def load_ecast():
+            nc.scalar.activation(out=e_f32[:], in_=e_bf[:], func=ACT.Copy)
+
+        loads = [lambda: load_a(0,1,0,2), load_e, lambda: load_a(0,1,2,4), lambda: load_a(1,1,0,4), load_small, load_ecast, lambda: load_x(0,0,2), lambda: load_x(0,2,4), lambda: load_a(2,1,0,4), lambda: load_a(3,1,0,4), lambda: load_d(0,0,1), lambda: load_a(4,1,0,4), lambda: load_a(5,1,0,4), lambda: load_a(6,2,0,4), lambda: load_d(1,0,1), lambda: load_x(1,0,4), lambda: load_a(8,2,0,4), lambda: load_d(0,1,2), lambda: load_d(1,1,2), lambda: load_a(10,2,0,4), lambda: load_a(12,2,0,4), lambda: load_d(2,0,2), lambda: load_a(14,2,0,4), lambda: load_d(3,0,2)]
+
+        def issue_loads(count):
+            for n in range(min(count, len(loads))):
+                loads.pop(0)()
+
+        sorted_words = {}
+        a_codes = {}
+        a_plane = {}
+        ed = {}
+        y = {}
+        fillers = []
+
+        def sort_words(j):
+            tile = work.tile([P, PASSES, 2, P], F32, name="sorted", bufs=3, align_bytes=64)
+            for kg0, kg1, eng in ((0, SORT_V, "v"), (SORT_V, PASSES, "s")):
+                for kg in range(kg0, kg1):
+                    sorted_words[(j, kg)] = tile[:, kg, :, :]
+                if kg1 > kg0:
+                    src = a_full[j][:, kg0 * 2 * P:kg1 * 2 * P].rearrange("m (k p u) -> m k u p", p=P, u=2)
+                    if eng == "v":
+                        nc.vector.tensor_copy(out=tile[:, kg0:kg1, :, :], in_=src)
+                    else:
+                        nc.scalar.copy(out=tile[:, kg0:kg1, :, :], in_=src)
+
+        def transpose_tile(j):
+            grouped = work.tile([P, PASSES * K_PASS], BF16, name="grouped", bufs=RUN + 2, align_bytes=64)
+            for half in range(2):
+                bank = psum.tile([P, 2, 2, P], F32, name="t_bank")
+                for kk in range(2):
+                    kg = 2 * half + kk
+                    for u in range(2):
+                        if (j, kg) in sorted_words:
+                            src = sorted_words[(j, kg)][:, u, :]
+                        else:
+                            src = a_words[(j, kg)][:, u::2]
+                        nc.tensor.transpose(bank[:, kk, u, :], src, ident[:])
+                dst = grouped[:, half * 2 * K_PASS:(half + 1) * 2 * K_PASS].bitcast(F32)
+                nc.scalar.copy(out=dst.rearrange("p (k m u) -> p k m u", k=2, u=2),
+                               in_=bank[:].rearrange("p k u m -> p k m u"))
+            return grouped
+
+        def quantize_a(j, grouped, pieces):
+            codes = work.tile([P, PASSES * P], I32, name="a_codes", bufs=10, align_bytes=64)
+            plane = work.tile([P, PASSES * P], U8, name="a_plane", bufs=10, align_bytes=64)
+            w = PASSES * P // pieces
+            for n in range(pieces):
+                nc.vector.quantize_mx(out=codes[:, n * w:(n + 1) * w].bitcast(FP8X4), scales=plane[:, n * w:(n + 1) * w],
+                                      in_=grouped[:, n * w * PACK:(n + 1) * w * PACK])
+            a_codes[j] = codes
+            a_plane[j] = plane
+
+        def scale_d(i):
+            u, t = groups[i]
+            g, c0, w = units[u]
+            h, off = divmod(c0, BANK)
+            tile = work.tile([P, w], F32, name="ed", bufs=ED_AHEAD + 2)
+            nc.scalar.activation(out=tile[:], in_=d_rows[(g, h)][:, t, off:off + w], func=ACT.Copy,
+                                 scale=e_f32[:, g, t:t + 1])
+            ed[i] = tile
+
+        def multiply(i):
+            u, t = groups[i]
+            g, c0, w = units[u]
+            h, off = divmod(c0, BANK)
+            j = PACK * g + t
+            acc = psum.tile([P, w], F32, name="acc", tag="t_bank" if i >= 27 and i % 2 else "acc")
+            for kg in range(PASSES):
+                nc.tensor.matmul_mx(
+                    out=acc[:],
+                    lhsT=a_codes[j][:, kg * P:(kg + 1) * P].bitcast(FP8X4),
+                    lhsT_scale=a_plane[j][:, kg * P:(kg + 1) * P],
+                    rhs=x_codes[(kg, h)][:, off:off + w].bitcast(FP8X4),
+                    rhs_scale=x_plane[4 * kg:P, c0:c0 + w],
+                    start=(kg == 0), stop=(kg == PASSES - 1))
+            return acc
+
+        def finish(i, acc):
+            u, t = groups[i]
+            g, c0, w = units[u]
+            if t == 0:
+                y[u] = work.tile([P, PACK, w], F32, name="y", bufs=5, align_bytes=64)
+            nc.vector.scalar_tensor_tensor(out=y[u][:, t, :], in0=acc[:], scalar=e_f32[:, g, t:t + 1], in1=ed[i][:],
+                                           op0=ALU.mult, op1=ALU.add)
+            dst = out_0[g * K_PASS:(g + 1) * K_PASS, c0:c0 + w].rearrange("(p t) c -> p t c", t=PACK)
+            if u >= TAIL_FROM:
+                if t % 2 == 1:
+                    nc.sync.dma_start(out=dst[:, t - 1:t + 1, :], in_=y[u][:, t - 1:t + 1, :])
+            elif t == PACK - 1:
+                nc.sync.dma_start(out=dst, in_=y[u][:])
+                issue_loads(LOADS_PER_STORE)
+
+        def interleave(eng, u, y_bf, lo, hi):
+            dst = y_bf[:, lo * PACK:hi * PACK].rearrange("p (c i t) -> p c t i", i=4, t=PACK)
+            src = y[u][:, :, lo:hi].rearrange("p t (c i) -> p c t i", i=4)
+            if eng == "v":
+                nc.vector.tensor_copy(out=dst, in_=src)
+            else:
+                nc.scalar.copy(out=dst, in_=src)
+
+        def quantize_y(u, y_bf):
+            g, c0, w = units[u]
+            codes = work.tile([P, w], I32, name="y_codes", bufs=5, align_bytes=64)
+            nc.vector.quantize_mx(out=codes[:].bitcast(FP8X4), scales=y_plane[4 * g:P, c0:c0 + w], in_=y_bf[:])
+            dst = out_1[g, :, c0:c0 + w, :].rearrange("p n t -> p (n t)")
+            nc.sync.dma_start(out=dst.bitcast(I32), in_=codes[:])
+
+        def queue_planes(u):
+            g, c0, w = units[u]
+            y_bf = work.tile([P, w * PACK], BF16, name="y_bf", bufs=2, align_bytes=64)
+            share = ILV_S[u] * w // 8
+            if share:
+                interleave("s", u, y_bf, w - share, w)
+            rest = w - share
+            if w == BANK and rest > 256:
+                fillers.append(lambda: interleave("v", u, y_bf, 0, rest // 2))
+                fillers.append(lambda: interleave("v", u, y_bf, rest // 2, rest))
+            elif rest:
+                fillers.append(lambda: interleave("v", u, y_bf, 0, rest))
+            for n in range([0,0,0,0,0,0,4,3,0,0][u]):
+                fillers.append(lambda: None)
+            fillers.append(lambda: quantize_y(u, y_bf))
+
+        def pop_filler():
+            if fillers:
+                fillers.pop(0)()
+
+        def epilogue(i, acc):
+            while len(ed) < i + 1:
+                scale_d(len(ed))
+            if i >= 17:
+                for n in range(2):
+                    if len(ed) < min(len(groups), i + 1 + ED_AHEAD):
+                        scale_d(len(ed))
+            finish(i, acc)
+            if groups[i][1] == PACK - 1:
+                queue_planes(groups[i][0])
+            pop_filler()
+
+        TAIL_FROM = 6
+        HEAD = 1
+        deferred = []
+        issue_loads(LOADS_FIRST)
+        before = [0,0,1,2,3,4,5,6,7,10,12,15,17,20,22,25]
+        runs = [[j] for j in range(16)]
+        sort_at = {}
+        for r in range(1, len(runs)):
+            sort_at[r - 1] = [j for j in runs[r] if j >= SORT_FROM]
+        run = 0
+        for i in range(len(groups)):
+            while run < len(runs) and before[run] <= i:
+                staged = [transpose_tile(j) for j in runs[run]]
+                for n, j in enumerate(runs[run]):
+                    pop_filler()
+                    quantize_a(j, staged[n], 2 if j == 0 else 1)
+                for j in sort_at.get(run, []):
+                    sort_words(j)
+                run = run + 1
+            if i >= HEAD:
+                while deferred:
+                    epilogue(*deferred.pop(0))
+            acc = multiply(i)
+            if i < HEAD:
+                deferred.append((i, acc))
+            else:
+                epilogue(i, acc)
+        while fillers:
+            pop_filler()
+        for q in range(4):
+            eng = nc.scalar if q % 2 else nc.sync
+            eng.dma_start(out=out_2[:, 4 * q:4 * q + 4, :].bitcast(I32), in_=y_plane[32 * q:32 * q + 16, :].bitcast(I32))

@@ -21,13 +21,13 @@ PASSES = S // K_PASS
 BANK = 512
 ROW_TILES = S // P
 
-SORT_FROM = 16
-SORT_V = 4
-RUN = 1
-ED_AHEAD = 6
-ILV_S = [0,0,0,0,0,0,6,8,3,3]
-LOADS_FIRST = 21
-LOADS_PER_STORE = 3
+SORT_FROM = 5
+SORT_V = 2
+RUN = 2
+ED_AHEAD = 3
+ILV_S = [0,0,0,0,0,0,4,6,3]
+LOADS_FIRST = 22
+LOADS_PER_STORE = 2
 
 
 def tile_sector_emission_changes_g6_kernel(tc, x_words, x_scales, a, d, e, out_0, out_1, out_2):
@@ -104,12 +104,12 @@ def tile_sector_emission_changes_g6_kernel(tc, x_words, x_scales, a, d, e, out_0
         y = {}
         fillers = []
 
-        def sort_words(j):
-            tile = work.tile([P, PASSES, 2, P], F32, name="sorted", bufs=3, align_bytes=64)
-            for kg0, kg1, eng in ((0, SORT_V, "v"), (SORT_V, PASSES, "s")):
+        def sort_words(j, tile, who):
+            sv, ss = (4, 0) if j < 8 else (SORT_V, 2)
+            for kg0, kg1, eng in ((0, sv, "v"), (sv, sv + ss, "s")):
                 for kg in range(kg0, kg1):
                     sorted_words[(j, kg)] = tile[:, kg, :, :]
-                if kg1 > kg0:
+                if kg1 > kg0 and eng == who:
                     src = a_full[j][:, kg0 * 2 * P:kg1 * 2 * P].rearrange("m (k p u) -> m k u p", p=P, u=2)
                     if eng == "v":
                         nc.vector.tensor_copy(out=tile[:, kg0:kg1, :, :], in_=src)
@@ -117,7 +117,7 @@ def tile_sector_emission_changes_g6_kernel(tc, x_words, x_scales, a, d, e, out_0
                         nc.scalar.copy(out=tile[:, kg0:kg1, :, :], in_=src)
 
         def transpose_tile(j):
-            grouped = work.tile([P, PASSES * K_PASS], BF16, name="grouped", bufs=RUN + 2, align_bytes=64)
+            grouped = work.tile([P, PASSES * K_PASS], BF16, name="grouped", bufs=4, align_bytes=64)
             for half in range(2):
                 bank = psum.tile([P, 2, 2, P], F32, name="t_bank")
                 for kk in range(2):
@@ -147,7 +147,7 @@ def tile_sector_emission_changes_g6_kernel(tc, x_words, x_scales, a, d, e, out_0
             u, t = groups[i]
             g, c0, w = units[u]
             h, off = divmod(c0, BANK)
-            tile = work.tile([P, w], F32, name="ed", bufs=ED_AHEAD + 2)
+            tile = work.tile([P, w], F32, name="ed_%d" % w, bufs=6 if w == BANK else 9)
             nc.scalar.activation(out=tile[:], in_=d_rows[(g, h)][:, t, off:off + w], func=ACT.Copy,
                                  scale=e_f32[:, g, t:t + 1])
             ed[i] = tile
@@ -172,7 +172,7 @@ def tile_sector_emission_changes_g6_kernel(tc, x_words, x_scales, a, d, e, out_0
             u, t = groups[i]
             g, c0, w = units[u]
             if t == 0:
-                y[u] = work.tile([P, PACK, w], F32, name="y", bufs=5, align_bytes=64)
+                y[u] = work.tile([P, PACK, w], F32, name="y", bufs=4, align_bytes=64)
             nc.vector.scalar_tensor_tensor(out=y[u][:, t, :], in0=acc[:], scalar=e_f32[:, g, t:t + 1], in1=ed[i][:],
                                            op0=ALU.mult, op1=ALU.add)
             dst = out_0[g * K_PASS:(g + 1) * K_PASS, c0:c0 + w].rearrange("(p t) c -> p t c", t=PACK)
@@ -193,7 +193,7 @@ def tile_sector_emission_changes_g6_kernel(tc, x_words, x_scales, a, d, e, out_0
 
         def quantize_y(u, y_bf):
             g, c0, w = units[u]
-            codes = work.tile([P, w], I32, name="y_codes", bufs=5, align_bytes=64)
+            codes = work.tile([P, w], I32, name="y_codes", bufs=4, align_bytes=64)
             nc.vector.quantize_mx(out=codes[:].bitcast(FP8X4), scales=y_plane[4 * g:P, c0:c0 + w], in_=y_bf[:])
             dst = out_1[g, :, c0:c0 + w, :].rearrange("p n t -> p (n t)")
             nc.sync.dma_start(out=dst.bitcast(I32), in_=codes[:])
@@ -206,52 +206,88 @@ def tile_sector_emission_changes_g6_kernel(tc, x_words, x_scales, a, d, e, out_0
                 interleave("s", u, y_bf, w - share, w)
             rest = w - share
             if w == BANK and rest > 256:
-                fillers.append(lambda: interleave("v", u, y_bf, 0, rest // 2))
-                fillers.append(lambda: interleave("v", u, y_bf, rest // 2, rest))
+                fillers.append(("ilv", u, lambda: interleave("v", u, y_bf, 0, rest // 2)))
+                fillers.append(("ilv", u, lambda: interleave("v", u, y_bf, rest // 2, rest)))
             elif rest:
-                fillers.append(lambda: interleave("v", u, y_bf, 0, rest))
-            for n in range([0,0,0,0,0,0,4,3,0,0][u]):
-                fillers.append(lambda: None)
-            fillers.append(lambda: quantize_y(u, y_bf))
+                fillers.append(("ilv", u, lambda: interleave("v", u, y_bf, 0, rest)))
+            for n in range([0,0,0,0,0,0,3,2,0][u]):
+                fillers.append(("none", u, lambda: None))
+            fillers.append(("qy", u, lambda: quantize_y(u, y_bf)))
+
+        last = [None]
+        s_later = []
 
         def pop_filler():
-            if fillers:
-                fillers.pop(0)()
+            for n, (kind, key, fn) in enumerate(fillers):
+                if (kind == "ilv" and last[0] == ("stt", key)) or (kind == "qy" and last[0] == ("ilv", key)):
+                    continue
+                if kind in ("qy", "none") and any(k2 in ("ilv", "none") and key2 == key for k2, key2, f2 in fillers[:n]):
+                    continue
+                fillers.pop(n)
+                fn()
+                if kind != "none":
+                    last[0] = (kind, key)
+                return
+
+        def force(kind, key):
+            for n, (k2, key2, fn) in enumerate(fillers):
+                if (k2, key2) == (kind, key):
+                    fillers.pop(n)
+                    fn()
+                    last[0] = (kind, key)
+                    return
 
         def epilogue(i, acc):
             while len(ed) < i + 1:
                 scale_d(len(ed))
-            if i >= 17:
+            if i >= 9:
                 for n in range(2):
-                    if len(ed) < min(len(groups), i + 1 + ED_AHEAD):
-                        scale_d(len(ed))
+                    if len(ed) < min(len(groups), i + 1 + (ED_AHEAD if i < before[-1] else 99)):
+                        if units[groups[len(ed)][0]][2] < BANK or len(ed) - i < 6 - 1:
+                            scale_d(len(ed))
+            if s_later:
+                s_later.pop(0)()
             finish(i, acc)
+            last[0] = ("stt", groups[i][0] if groups[i][1] == PACK - 1 else -1)
             if groups[i][1] == PACK - 1:
                 queue_planes(groups[i][0])
             pop_filler()
+            if len(fillers) >= 3:
+                pop_filler()
 
         TAIL_FROM = 6
         HEAD = 1
         deferred = []
         issue_loads(LOADS_FIRST)
-        before = [0,0,1,2,3,4,5,6,7,10,12,15,17,20,22,25]
-        runs = [[j] for j in range(16)]
+        before = [0,0,1,1,2,3,4,5,10,14,19,24]
+        runs = [[0],[1],[2],[3],[4],[5],[6],[7],[8,9],[10,11],[12,13],[14,15]]
         sort_at = {}
         for r in range(1, len(runs)):
-            sort_at[r - 1] = [j for j in runs[r] if j >= SORT_FROM]
+            sort_at.setdefault(r - (2 if len(runs[r]) == 1 else 1), []).extend([j for j in runs[r] if j >= SORT_FROM])
         run = 0
         for i in range(len(groups)):
             while run < len(runs) and before[run] <= i:
+                for j in runs[run]:
+                    force("sort", j)
+                while s_later and 2 == 1:
+                    s_later.pop(0)()
                 staged = [transpose_tile(j) for j in runs[run]]
-                for n, j in enumerate(runs[run]):
+                for n in range(1):
                     pop_filler()
-                    quantize_a(j, staged[n], 2 if j == 0 else 1)
+                quantize_a(runs[run][0], staged[0], 2 if run == 0 else 1)
+                last[0] = None
+                front = [("qa", j, lambda j=j, src=staged[n]: quantize_a(j, src, 1)) for n, j in enumerate(runs[run]) if n > 0]
                 for j in sort_at.get(run, []):
-                    sort_words(j)
+                    dst = work.tile([P, PASSES, 2, P], F32, name="sorted", bufs=3, align_bytes=64)
+                    s_later.append(lambda j=j, dst=dst: sort_words(j, dst, "s"))
+                    front.append(("sort", j, lambda j=j, dst=dst: sort_words(j, dst, "v")))
+                for n, item in enumerate(front):
+                    fillers.insert(n if item[0] == "qa" or 1 else len(fillers), item)
                 run = run + 1
             if i >= HEAD:
                 while deferred:
                     epilogue(*deferred.pop(0))
+            force("qa", PACK * units[groups[i][0]][0] + groups[i][1])
             acc = multiply(i)
             if i < HEAD:
                 deferred.append((i, acc))
@@ -259,6 +295,7 @@ def tile_sector_emission_changes_g6_kernel(tc, x_words, x_scales, a, d, e, out_0
                 epilogue(i, acc)
         while fillers:
             pop_filler()
+            last[0] = None
         for q in range(4):
             eng = nc.scalar if q % 2 else nc.sync
             eng.dma_start(out=out_2[:, 4 * q:4 * q + 4, :].bitcast(I32), in_=y_plane[32 * q:32 * q + 16, :].bitcast(I32))

@@ -18,103 +18,114 @@ P = 128
 PACK = 4
 K_PASS = P * PACK
 PASSES = S // K_PASS
-BANK = 512
 ROW_TILES = S // P
+BANK = 512
+QUADRANTS = 4
 
+UNITS = [(0, 0, BANK), (1, 0, BANK), (0, BANK, BANK), (1, BANK, BANK), (2, 0, BANK), (2, BANK, BANK), (3, 0, BANK),
+         (3, BANK, BANK // 2), (3, BANK + BANK // 2, BANK // 2)]
+GROUPS = [(u, t) for u in range(len(UNITS)) for t in range(PACK)]
+OPENING = 2 * PACK
+
+LEAD = 2
+RUN_EVERY = 5
 SORT_FROM = 5
-SORT_V = 2
-RUN = 2
 ED_AHEAD = 3
-ILV_S = [0,0,0,0,0,0,4,6,3]
-LOADS_FIRST = 22
-LOADS_PER_STORE = 2
+BACKLOG = 3
+SHARE = 5
+SHARE_LAST = 3
+PAUSE = 4
+
+
+def transpose_runs():
+    runs = [(max(0, j - LEAD), [j]) for j in range(OPENING)]
+    last_use = GROUPS.index((UNITS.index((PASSES - 1, 0, BANK)), 2))
+    doubles = list(range(OPENING, ROW_TILES, 2))
+    for n, j in enumerate(doubles):
+        runs.append((last_use - LEAD - RUN_EVERY * (len(doubles) - 1 - n), [j, j + 1]))
+    return runs
 
 
 def tile_sector_emission_changes_g6_kernel(tc, x_words, x_scales, a, d, e, out_0, out_1, out_2):
     nc = tc.nc
-    units = [(0, 0, 512), (1, 0, 512), (0, 512, 512), (1, 512, 512), (2, 0, 512), (2, 512, 512), (3, 0, 512), (3, 512, 256), (3, 768, 256)]
-    groups = [(u, t) for u in range(len(units)) for t in range(PACK)]
+    runs = transpose_runs()
+    last_run_at = runs[-1][0]
 
     with ExitStack() as ctx:
         keep = ctx.enter_context(tc.tile_pool(name="keep", bufs=1))
         work = ctx.enter_context(tc.tile_pool(name="work", bufs=2))
         psum = ctx.enter_context(tc.psum_pool(name="psum", bufs=4))
-
-        ident = keep.tile([P, P], F32, name="ident")
-        make_identity(nc, ident[:])
         ctx.enter_context(tc.manual_schedule())
 
         x_plane = keep.tile([P, M], U8, name="x_plane", align_bytes=64)
+        nc.gpsimd.memset(x_plane[:].bitcast(I32), 0)
+        ident = keep.tile([P, P], F32, name="ident")
+        make_identity(nc, ident[:])
         y_plane = keep.tile([P, M], U8, name="y_plane", align_bytes=64)
         e_bf = keep.tile([P, PASSES, PACK], BF16, name="e_bf")
         e_f32 = keep.tile([P, PASSES, PACK], F32, name="e_f32")
-        nc.vector.memset(x_plane[:].bitcast(I32), 0)
 
-        a_words = {}
-        a_full = {}
+        a_pairs = {}
+        a_rows = {}
         x_codes = {}
         d_rows = {}
 
-        def load_a(j0, count, kg0, kg1):
+        def load_a(j0, count, kg0=0, kg1=PASSES):
             g, t0 = divmod(j0, PACK)
-            tile = keep.tile([P, count, (kg1 - kg0) * K_PASS], BF16, name="a_%d_%d" % (j0, kg0), align_bytes=64)
+            a_sb = keep.tile([P, count, (kg1 - kg0) * K_PASS], BF16, name="a_%d_%d" % (j0, kg0), align_bytes=64)
             rows = a[g * K_PASS:(g + 1) * K_PASS, kg0 * K_PASS:kg1 * K_PASS].rearrange("(m t) k -> m t k", t=PACK)
-            nc.sync.dma_start(out=tile[:], in_=rows[:, t0:t0 + count, :])
+            nc.sync.dma_start(out=a_sb[:], in_=rows[:, t0:t0 + count, :])
             for n in range(count):
-                words = tile[:, n, :].bitcast(F32)
-                a_full[j0 + n] = words
+                a_rows[j0 + n] = a_sb[:, n, :].bitcast(F32)
                 for kg in range(kg0, kg1):
-                    a_words[(j0 + n, kg)] = words[:, (kg - kg0) * 2 * P:(kg - kg0 + 1) * 2 * P]
+                    a_pairs[(j0 + n, kg)] = a_rows[j0 + n][:, (kg - kg0) * 2 * P:(kg - kg0 + 1) * 2 * P]
 
         def load_x(h, kg0, kg1):
-            tile = keep.tile([P, kg1 - kg0, BANK], I32, name="x_%d_%d" % (h, kg0), align_bytes=64)
+            x_sb = keep.tile([P, kg1 - kg0, BANK], I32, name="x_%d_%d" % (h, kg0), align_bytes=64)
             src = x_words[kg0:kg1, :, h * BANK:(h + 1) * BANK, :].rearrange("g p n t -> p g (n t)")
-            nc.sync.dma_start(out=tile[:], in_=src.bitcast(I32))
+            nc.sync.dma_start(out=x_sb[:], in_=src.bitcast(I32))
             for kg in range(kg0, kg1):
-                x_codes[(kg, h)] = tile[:, kg - kg0, :]
+                x_codes[(kg, h)] = x_sb[:, kg - kg0, :]
 
         def load_d(g, h0, h1):
-            tile = keep.tile([P, PACK, (h1 - h0) * BANK], BF16, name="d_%d_%d" % (g, h0))
+            d_sb = keep.tile([P, PACK, (h1 - h0) * BANK], BF16, name="d_%d_%d" % (g, h0))
             src = d[g * K_PASS:(g + 1) * K_PASS, h0 * BANK:h1 * BANK].rearrange("(p t) c -> p t c", t=PACK)
-            nc.sync.dma_start(out=tile[:], in_=src)
+            nc.sync.dma_start(out=d_sb[:], in_=src)
             for h in range(h0, h1):
-                d_rows[(g, h)] = tile[:, :, (h - h0) * BANK:(h - h0 + 1) * BANK]
+                d_rows[(g, h)] = d_sb[:, :, (h - h0) * BANK:(h - h0 + 1) * BANK]
 
-        def load_small():
-            for q in range(4):
-                nc.scalar.dma_start(out=x_plane[32 * q:32 * q + 16, :].bitcast(I32),
-                                    in_=x_scales[:, 4 * q:4 * q + 4, :].bitcast(I32))
+        load_a(0, 1, 0, 2)
+        nc.scalar.dma_start(out=e_bf[:], in_=e.rearrange("(g p t) -> p g t", p=P, t=PACK))
+        load_a(0, 1, 2, 4)
+        load_a(1, 1)
+        for q in range(QUADRANTS):
+            nc.scalar.dma_start(out=x_plane[32 * q:32 * q + 16, :].bitcast(I32),
+                                in_=x_scales[:, 4 * q:4 * q + 4, :].bitcast(I32))
+        nc.scalar.activation(out=e_f32[:], in_=e_bf[:], func=ACT.Copy)
+        load_a(2, 1)
+        load_x(0, 0, 2)
+        load_x(0, 2, 4)
+        load_a(3, 1)
+        load_a(4, 1)
+        load_d(0, 0, 1)
+        load_a(5, 1)
+        load_a(6, 2)
+        load_d(1, 0, 1)
+        load_x(1, 0, 4)
+        load_a(8, 2)
+        load_d(0, 1, 2)
+        load_d(1, 1, 2)
+        load_a(10, 2)
+        load_a(12, 2)
+        load_d(2, 0, 2)
 
-        def load_e():
-            nc.scalar.dma_start(out=e_bf[:], in_=e.rearrange("(g p t) -> p g t", p=P, t=PACK))
-
-        def load_ecast():
-            nc.scalar.activation(out=e_f32[:], in_=e_bf[:], func=ACT.Copy)
-
-        loads = [lambda: load_a(0,1,0,2), load_e, lambda: load_a(0,1,2,4), lambda: load_a(1,1,0,4), load_small, load_ecast, lambda: load_x(0,0,2), lambda: load_x(0,2,4), lambda: load_a(2,1,0,4), lambda: load_a(3,1,0,4), lambda: load_d(0,0,1), lambda: load_a(4,1,0,4), lambda: load_a(5,1,0,4), lambda: load_a(6,2,0,4), lambda: load_d(1,0,1), lambda: load_x(1,0,4), lambda: load_a(8,2,0,4), lambda: load_d(0,1,2), lambda: load_d(1,1,2), lambda: load_a(10,2,0,4), lambda: load_a(12,2,0,4), lambda: load_d(2,0,2), lambda: load_a(14,2,0,4), lambda: load_d(3,0,2)]
-
-        def issue_loads(count):
-            for n in range(min(count, len(loads))):
-                loads.pop(0)()
-
-        sorted_words = {}
+        sorted_pairs = {}
         a_codes = {}
         a_plane = {}
-        ed = {}
-        y = {}
-        fillers = []
 
-        def sort_words(j, tile, who):
-            sv, ss = (4, 0) if j < 8 else (SORT_V, 2)
-            for kg0, kg1, eng in ((0, sv, "v"), (sv, sv + ss, "s")):
-                for kg in range(kg0, kg1):
-                    sorted_words[(j, kg)] = tile[:, kg, :, :]
-                if kg1 > kg0 and eng == who:
-                    src = a_full[j][:, kg0 * 2 * P:kg1 * 2 * P].rearrange("m (k p u) -> m k u p", p=P, u=2)
-                    if eng == "v":
-                        nc.vector.tensor_copy(out=tile[:, kg0:kg1, :, :], in_=src)
-                    else:
-                        nc.scalar.copy(out=tile[:, kg0:kg1, :, :], in_=src)
+        def sort_pairs(copy, j, kg0, kg1):
+            src = a_rows[j][:, kg0 * 2 * P:kg1 * 2 * P].rearrange("m (k p u) -> m k u p", p=P, u=2)
+            copy(out=sorted_pairs[j][:, kg0:kg1, :, :], in_=src)
 
         def transpose_tile(j):
             grouped = work.tile([P, PASSES * K_PASS], BF16, name="grouped", bufs=4, align_bytes=64)
@@ -123,41 +134,42 @@ def tile_sector_emission_changes_g6_kernel(tc, x_words, x_scales, a, d, e, out_0
                 for kk in range(2):
                     kg = 2 * half + kk
                     for u in range(2):
-                        if (j, kg) in sorted_words:
-                            src = sorted_words[(j, kg)][:, u, :]
-                        else:
-                            src = a_words[(j, kg)][:, u::2]
+                        src = sorted_pairs[j][:, kg, u, :] if j >= SORT_FROM else a_pairs[(j, kg)][:, u::2]
                         nc.tensor.transpose(bank[:, kk, u, :], src, ident[:])
                 dst = grouped[:, half * 2 * K_PASS:(half + 1) * 2 * K_PASS].bitcast(F32)
                 nc.scalar.copy(out=dst.rearrange("p (k m u) -> p k m u", k=2, u=2),
                                in_=bank[:].rearrange("p k u m -> p k m u"))
             return grouped
 
-        def quantize_a(j, grouped, pieces):
-            codes = work.tile([P, PASSES * P], I32, name="a_codes", bufs=10, align_bytes=64)
-            plane = work.tile([P, PASSES * P], U8, name="a_plane", bufs=10, align_bytes=64)
+        def quantize_a(j, grouped):
+            a_codes[j] = work.tile([P, PASSES * P], I32, name="a_codes", bufs=10, align_bytes=64)
+            a_plane[j] = work.tile([P, PASSES * P], U8, name="a_plane", bufs=10, align_bytes=64)
+            pieces = 2 if j == 0 else 1
             w = PASSES * P // pieces
             for n in range(pieces):
-                nc.vector.quantize_mx(out=codes[:, n * w:(n + 1) * w].bitcast(FP8X4), scales=plane[:, n * w:(n + 1) * w],
+                nc.vector.quantize_mx(out=a_codes[j][:, n * w:(n + 1) * w].bitcast(FP8X4),
+                                      scales=a_plane[j][:, n * w:(n + 1) * w],
                                       in_=grouped[:, n * w * PACK:(n + 1) * w * PACK])
-            a_codes[j] = codes
-            a_plane[j] = plane
 
-        def scale_d(i):
-            u, t = groups[i]
-            g, c0, w = units[u]
+        ed = []
+        y = {}
+
+        def scale_d():
+            u, t = GROUPS[len(ed)]
+            g, c0, w = UNITS[u]
             h, off = divmod(c0, BANK)
-            tile = work.tile([P, w], F32, name="ed_%d" % w, bufs=6 if w == BANK else 9)
-            nc.scalar.activation(out=tile[:], in_=d_rows[(g, h)][:, t, off:off + w], func=ACT.Copy,
+            ed_sb = work.tile([P, w], F32, name="ed_%d" % w, bufs=ED_AHEAD + 3 if w == BANK else 2 * PACK)
+            nc.scalar.activation(out=ed_sb[:], in_=d_rows[(g, h)][:, t, off:off + w], func=ACT.Copy,
                                  scale=e_f32[:, g, t:t + 1])
-            ed[i] = tile
+            ed.append(ed_sb)
 
         def multiply(i):
-            u, t = groups[i]
-            g, c0, w = units[u]
+            u, t = GROUPS[i]
+            g, c0, w = UNITS[u]
             h, off = divmod(c0, BANK)
             j = PACK * g + t
-            acc = psum.tile([P, w], F32, name="acc", tag="t_bank" if i >= 27 and i % 2 else "acc")
+            spare = i >= len(GROUPS) - 2 * PACK - 1 and i % 2 == 1
+            acc = psum.tile([P, w], F32, name="acc", tag="t_bank" if spare else "acc")
             for kg in range(PASSES):
                 nc.tensor.matmul_mx(
                     out=acc[:],
@@ -168,134 +180,125 @@ def tile_sector_emission_changes_g6_kernel(tc, x_words, x_scales, a, d, e, out_0
                     start=(kg == 0), stop=(kg == PASSES - 1))
             return acc
 
-        def finish(i, acc):
-            u, t = groups[i]
-            g, c0, w = units[u]
+        def add_and_store(i, acc):
+            u, t = GROUPS[i]
+            g, c0, w = UNITS[u]
             if t == 0:
                 y[u] = work.tile([P, PACK, w], F32, name="y", bufs=4, align_bytes=64)
             nc.vector.scalar_tensor_tensor(out=y[u][:, t, :], in0=acc[:], scalar=e_f32[:, g, t:t + 1], in1=ed[i][:],
                                            op0=ALU.mult, op1=ALU.add)
             dst = out_0[g * K_PASS:(g + 1) * K_PASS, c0:c0 + w].rearrange("(p t) c -> p t c", t=PACK)
-            if u >= TAIL_FROM:
+            if g == PASSES - 1:
                 if t % 2 == 1:
                     nc.sync.dma_start(out=dst[:, t - 1:t + 1, :], in_=y[u][:, t - 1:t + 1, :])
             elif t == PACK - 1:
                 nc.sync.dma_start(out=dst, in_=y[u][:])
-                issue_loads(LOADS_PER_STORE)
+                if u == 0:
+                    load_a(ROW_TILES - 2, 2)
+                    load_d(PASSES - 1, 0, 2)
 
-        def interleave(eng, u, y_bf, lo, hi):
-            dst = y_bf[:, lo * PACK:hi * PACK].rearrange("p (c i t) -> p c t i", i=4, t=PACK)
-            src = y[u][:, :, lo:hi].rearrange("p t (c i) -> p c t i", i=4)
-            if eng == "v":
-                nc.vector.tensor_copy(out=dst, in_=src)
-            else:
-                nc.scalar.copy(out=dst, in_=src)
+        def interleave(copy, u, y_bf, lo, hi):
+            copy(out=y_bf[:, lo * PACK:hi * PACK].rearrange("p (c i t) -> p c t i", i=4, t=PACK),
+                 in_=y[u][:, :, lo:hi].rearrange("p t (c i) -> p c t i", i=4))
 
         def quantize_y(u, y_bf):
-            g, c0, w = units[u]
-            codes = work.tile([P, w], I32, name="y_codes", bufs=4, align_bytes=64)
-            nc.vector.quantize_mx(out=codes[:].bitcast(FP8X4), scales=y_plane[4 * g:P, c0:c0 + w], in_=y_bf[:])
+            g, c0, w = UNITS[u]
+            y_codes = work.tile([P, w], I32, name="y_codes", bufs=4, align_bytes=64)
+            nc.vector.quantize_mx(out=y_codes[:].bitcast(FP8X4), scales=y_plane[4 * g:P, c0:c0 + w], in_=y_bf[:])
             dst = out_1[g, :, c0:c0 + w, :].rearrange("p n t -> p (n t)")
-            nc.sync.dma_start(out=dst.bitcast(I32), in_=codes[:])
+            nc.sync.dma_start(out=dst.bitcast(I32), in_=y_codes[:])
 
-        def queue_planes(u):
-            g, c0, w = units[u]
-            y_bf = work.tile([P, w * PACK], BF16, name="y_bf", bufs=2, align_bytes=64)
-            share = ILV_S[u] * w // 8
-            if share:
-                interleave("s", u, y_bf, w - share, w)
-            rest = w - share
-            if w == BANK and rest > 256:
-                fillers.append(("ilv", u, lambda: interleave("v", u, y_bf, 0, rest // 2)))
-                fillers.append(("ilv", u, lambda: interleave("v", u, y_bf, rest // 2, rest)))
-            elif rest:
-                fillers.append(("ilv", u, lambda: interleave("v", u, y_bf, 0, rest)))
-            for n in range([0,0,0,0,0,0,3,2,0][u]):
-                fillers.append(("none", u, lambda: None))
-            fillers.append(("qy", u, lambda: quantize_y(u, y_bf)))
+        vector_tasks = []
+        scalar_tasks = []
+        previous = [None]
 
-        last = [None]
-        s_later = []
-
-        def pop_filler():
-            for n, (kind, key, fn) in enumerate(fillers):
-                if (kind == "ilv" and last[0] == ("stt", key)) or (kind == "qy" and last[0] == ("ilv", key)):
+        def vector_turn():
+            for n, (kind, key, call) in enumerate(vector_tasks):
+                earlier = [(k, other) for k, other, unused in vector_tasks[:n]]
+                if kind == "interleave" and previous[0] == ("last add", key):
                     continue
-                if kind in ("qy", "none") and any(k2 in ("ilv", "none") and key2 == key for k2, key2, f2 in fillers[:n]):
+                if kind == "quantize y" and previous[0] == ("interleave", key):
                     continue
-                fillers.pop(n)
-                fn()
-                if kind != "none":
-                    last[0] = (kind, key)
+                if kind in ("pause", "quantize y") and (("interleave", key) in earlier or ("pause", key) in earlier):
+                    continue
+                vector_tasks.pop(n)
+                if kind != "pause":
+                    call()
+                    previous[0] = (kind, key)
                 return
 
-        def force(kind, key):
-            for n, (k2, key2, fn) in enumerate(fillers):
-                if (k2, key2) == (kind, key):
-                    fillers.pop(n)
-                    fn()
-                    last[0] = (kind, key)
-                    return
+        def plan_planes(u):
+            w = UNITS[u][2]
+            y_bf = work.tile([P, w * PACK], BF16, name="y_bf", bufs=2, align_bytes=64)
+            is_last = u == len(UNITS) - 1
+            shared = PACK * (u + 1) >= last_run_at
+            mine = w - (SHARE_LAST if is_last else SHARE) * w // 8 if shared else w
+            if PACK * (u + 1) == last_run_at:
+                scalar_tasks.append(lambda: interleave(nc.scalar.copy, u, y_bf, mine, w))
+            elif shared:
+                interleave(nc.scalar.copy, u, y_bf, mine, w)
+            cuts = [0, mine] if shared else [0, w // 2, w]
+            for lo, hi in zip(cuts, cuts[1:]):
+                vector_tasks.append(("interleave", u, lambda lo=lo, hi=hi: interleave(nc.vector.tensor_copy, u, y_bf, lo, hi)))
+            if shared and not is_last:
+                vector_tasks.extend([("pause", u, None)] * PAUSE)
+            vector_tasks.append(("quantize y", u, lambda: quantize_y(u, y_bf)))
+
+        def plan_sort(j):
+            sorted_pairs[j] = work.tile([P, PASSES, 2, P], F32, name="sorted", bufs=3, align_bytes=64)
+            mine = PASSES if j < OPENING else PASSES // 2
+            if mine < PASSES:
+                scalar_tasks.append(lambda: sort_pairs(nc.scalar.copy, j, mine, PASSES))
+            return ("sort", j, lambda: sort_pairs(nc.vector.tensor_copy, j, 0, mine))
+
+        def do_run(r):
+            tiles = runs[r][1]
+            staged = [transpose_tile(j) for j in tiles]
+            vector_turn()
+            quantize_a(tiles[0], staged[0])
+            previous[0] = None
+            urgent = [("quantize a", j, lambda j=j, src=src: quantize_a(j, src)) for j, src in zip(tiles[1:], staged[1:])]
+            for later in range(r + 1, len(runs)):
+                if later - r == (2 if len(runs[later][1]) == 1 else 1):
+                    urgent.extend([plan_sort(j) for j in runs[later][1] if j >= SORT_FROM])
+            for n, task in enumerate(urgent):
+                vector_tasks.insert(n, task)
 
         def epilogue(i, acc):
-            while len(ed) < i + 1:
-                scale_d(len(ed))
-            if i >= 9:
-                for n in range(2):
-                    if len(ed) < min(len(groups), i + 1 + (ED_AHEAD if i < before[-1] else 99)):
-                        if units[groups[len(ed)][0]][2] < BANK or len(ed) - i < 6 - 1:
-                            scale_d(len(ed))
-            if s_later:
-                s_later.pop(0)()
-            finish(i, acc)
-            last[0] = ("stt", groups[i][0] if groups[i][1] == PACK - 1 else -1)
-            if groups[i][1] == PACK - 1:
-                queue_planes(groups[i][0])
-            pop_filler()
-            if len(fillers) >= 3:
-                pop_filler()
+            u, t = GROUPS[i]
+            while len(ed) <= i:
+                scale_d()
+            if i >= OPENING:
+                target = i + 1 + ED_AHEAD if i < last_run_at else len(GROUPS)
+                for n in range(min(2, target - len(ed))):
+                    scale_d()
+            if scalar_tasks:
+                scalar_tasks.pop(0)()
+            add_and_store(i, acc)
+            previous[0] = ("last add", u) if t == PACK - 1 else None
+            if t == PACK - 1:
+                plan_planes(u)
+            vector_turn()
+            if i >= OPENING and len(vector_tasks) >= BACKLOG:
+                vector_turn()
 
-        TAIL_FROM = 6
-        HEAD = 1
-        deferred = []
-        issue_loads(LOADS_FIRST)
-        before = [0,0,1,1,2,3,4,5,10,14,19,24]
-        runs = [[0],[1],[2],[3],[4],[5],[6],[7],[8,9],[10,11],[12,13],[14,15]]
-        sort_at = {}
-        for r in range(1, len(runs)):
-            sort_at.setdefault(r - (2 if len(runs[r]) == 1 else 1), []).extend([j for j in runs[r] if j >= SORT_FROM])
-        run = 0
-        for i in range(len(groups)):
-            while run < len(runs) and before[run] <= i:
-                for j in runs[run]:
-                    force("sort", j)
-                while s_later and 2 == 1:
-                    s_later.pop(0)()
-                staged = [transpose_tile(j) for j in runs[run]]
-                for n in range(1):
-                    pop_filler()
-                quantize_a(runs[run][0], staged[0], 2 if run == 0 else 1)
-                last[0] = None
-                front = [("qa", j, lambda j=j, src=staged[n]: quantize_a(j, src, 1)) for n, j in enumerate(runs[run]) if n > 0]
-                for j in sort_at.get(run, []):
-                    dst = work.tile([P, PASSES, 2, P], F32, name="sorted", bufs=3, align_bytes=64)
-                    s_later.append(lambda j=j, dst=dst: sort_words(j, dst, "s"))
-                    front.append(("sort", j, lambda j=j, dst=dst: sort_words(j, dst, "v")))
-                for n, item in enumerate(front):
-                    fillers.insert(n if item[0] == "qa" or 1 else len(fillers), item)
-                run = run + 1
-            if i >= HEAD:
-                while deferred:
-                    epilogue(*deferred.pop(0))
-            force("qa", PACK * units[groups[i][0]][0] + groups[i][1])
+        next_run = 0
+        first = None
+        for i in range(len(GROUPS)):
+            while next_run < len(runs) and runs[next_run][0] <= i:
+                do_run(next_run)
+                next_run = next_run + 1
+            if i == 1:
+                epilogue(0, first)
             acc = multiply(i)
-            if i < HEAD:
-                deferred.append((i, acc))
+            if i == 0:
+                first = acc
             else:
                 epilogue(i, acc)
-        while fillers:
-            pop_filler()
-            last[0] = None
-        for q in range(4):
-            eng = nc.scalar if q % 2 else nc.sync
-            eng.dma_start(out=out_2[:, 4 * q:4 * q + 4, :].bitcast(I32), in_=y_plane[32 * q:32 * q + 16, :].bitcast(I32))
+        while vector_tasks:
+            vector_turn()
+            previous[0] = None
+        for q in range(QUADRANTS):
+            queue = nc.scalar if q % 2 else nc.sync
+            queue.dma_start(out=out_2[:, 4 * q:4 * q + 4, :].bitcast(I32),
+                            in_=y_plane[32 * q:32 * q + 16, :].bitcast(I32))

@@ -72,7 +72,9 @@ def tile_sector_emission_changes_g6_kernel(tc, x_words, x_scales, a, d, e, out_0
 
         def load_a(j0, count, kg0=0, kg1=PASSES):
             g, t0 = divmod(j0, PACK)
-            a_sb = keep.tile([P, count, (kg1 - kg0) * K_PASS], BF16, name="a_%d_%d" % (j0, kg0), align_bytes=64)
+            tag = "a_double" if count == 2 else "a_%d_%d" % (j0, kg0)
+            a_sb = keep.tile([P, count, (kg1 - kg0) * K_PASS], BF16, name=tag, bufs=3 if count == 2 else 1,
+                             align_bytes=64)
             rows = a[g * K_PASS:(g + 1) * K_PASS, kg0 * K_PASS:kg1 * K_PASS].rearrange("(m t) k -> m t k", t=PACK)
             nc.sync.dma_start(out=a_sb[:], in_=rows[:, t0:t0 + count, :])
             for n in range(count):
@@ -87,7 +89,7 @@ def tile_sector_emission_changes_g6_kernel(tc, x_words, x_scales, a, d, e, out_0
             for kg in range(kg0, kg1):
                 x_codes[(kg, h)] = x_sb[:, kg - kg0, :]
 
-        def load_d(g, h0, h1):
+        def load_d(g, h0=0, h1=2):
             d_sb = keep.tile([P, PACK, (h1 - h0) * BANK], BF16, name="d_%d_%d" % (g, h0))
             src = d[g * K_PASS:(g + 1) * K_PASS, h0 * BANK:h1 * BANK].rearrange("(p t) c -> p t c", t=PACK)
             nc.sync.dma_start(out=d_sb[:], in_=src)
@@ -116,8 +118,7 @@ def tile_sector_emission_changes_g6_kernel(tc, x_words, x_scales, a, d, e, out_0
         load_d(0, 1, 2)
         load_d(1, 1, 2)
         load_a(10, 2)
-        load_a(12, 2)
-        load_d(2, 0, 2)
+        load_d(2)
 
         sorted_pairs = {}
         a_codes = {}
@@ -153,12 +154,13 @@ def tile_sector_emission_changes_g6_kernel(tc, x_words, x_scales, a, d, e, out_0
 
         ed = []
         y = {}
+        y_codes = {}
 
         def scale_d():
             u, t = GROUPS[len(ed)]
             g, c0, w = UNITS[u]
             h, off = divmod(c0, BANK)
-            ed_sb = work.tile([P, w], F32, name="ed_%d" % w, bufs=ED_AHEAD + 3 if w == BANK else 2 * PACK)
+            ed_sb = work.tile([P, w], F32, name="ed_%d" % w, bufs=ED_AHEAD + 2 if w == BANK else 2 * PACK)
             nc.scalar.activation(out=ed_sb[:], in_=d_rows[(g, h)][:, t, off:off + w], func=ACT.Copy,
                                  scale=e_f32[:, g, t:t + 1])
             ed.append(ed_sb)
@@ -183,30 +185,30 @@ def tile_sector_emission_changes_g6_kernel(tc, x_words, x_scales, a, d, e, out_0
         def add_and_store(i, acc):
             u, t = GROUPS[i]
             g, c0, w = UNITS[u]
-            if t == 0:
-                y[u] = work.tile([P, PACK, w], F32, name="y", bufs=4, align_bytes=64)
-            nc.vector.scalar_tensor_tensor(out=y[u][:, t, :], in0=acc[:], scalar=e_f32[:, g, t:t + 1], in1=ed[i][:],
-                                           op0=ALU.mult, op1=ALU.add)
-            dst = out_0[g * K_PASS:(g + 1) * K_PASS, c0:c0 + w].rearrange("(p t) c -> p t c", t=PACK)
-            if g == PASSES - 1:
-                if t % 2 == 1:
-                    nc.sync.dma_start(out=dst[:, t - 1:t + 1, :], in_=y[u][:, t - 1:t + 1, :])
-            elif t == PACK - 1:
-                nc.sync.dma_start(out=dst, in_=y[u][:])
-                if u == 0:
-                    load_a(ROW_TILES - 2, 2)
-                    load_d(PASSES - 1, 0, 2)
+            if g not in y:
+                y[g] = work.tile([P, PACK, M], F32, name="y", bufs=3, align_bytes=64)
+            nc.vector.scalar_tensor_tensor(out=y[g][:, t, c0:c0 + w], in0=acc[:], scalar=e_f32[:, g, t:t + 1],
+                                           in1=ed[i][:], op0=ALU.mult, op1=ALU.add)
+            lo = c0 if g == PASSES - 1 else 0
+            if t % 2 == 1 and (g == PASSES - 1 or c0 > 0):
+                dst = out_0[g * K_PASS:(g + 1) * K_PASS, :].rearrange("(p t) c -> p t c", t=PACK)
+                nc.sync.dma_start(out=dst[:, t - 1:t + 1, lo:c0 + w], in_=y[g][:, t - 1:t + 1, lo:c0 + w])
 
         def interleave(copy, u, y_bf, lo, hi):
+            g, c0, w = UNITS[u]
             copy(out=y_bf[:, lo * PACK:hi * PACK].rearrange("p (c i t) -> p c t i", i=4, t=PACK),
-                 in_=y[u][:, :, lo:hi].rearrange("p t (c i) -> p c t i", i=4))
+                 in_=y[g][:, :, c0 + lo:c0 + hi].rearrange("p t (c i) -> p c t i", i=4))
 
         def quantize_y(u, y_bf):
             g, c0, w = UNITS[u]
-            y_codes = work.tile([P, w], I32, name="y_codes", bufs=4, align_bytes=64)
-            nc.vector.quantize_mx(out=y_codes[:].bitcast(FP8X4), scales=y_plane[4 * g:P, c0:c0 + w], in_=y_bf[:])
-            dst = out_1[g, :, c0:c0 + w, :].rearrange("p n t -> p (n t)")
-            nc.sync.dma_start(out=dst.bitcast(I32), in_=y_codes[:])
+            if g not in y_codes:
+                y_codes[g] = work.tile([P, M], I32, name="y_codes", bufs=2, align_bytes=64)
+            nc.vector.quantize_mx(out=y_codes[g][:, c0:c0 + w].bitcast(FP8X4), scales=y_plane[4 * g:P, c0:c0 + w],
+                                  in_=y_bf[:])
+            lo = c0 if g == PASSES - 1 else 0
+            if g == PASSES - 1 or c0 > 0:
+                dst = out_1[g, :, lo:c0 + w, :].rearrange("p n t -> p (n t)")
+                nc.sync.dma_start(out=dst.bitcast(I32), in_=y_codes[g][:, lo:c0 + w])
 
         vector_tasks = []
         scalar_tasks = []
@@ -274,6 +276,10 @@ def tile_sector_emission_changes_g6_kernel(tc, x_words, x_scales, a, d, e, out_0
                     scale_d()
             if scalar_tasks:
                 scalar_tasks.pop(0)()
+            if i == OPENING:
+                load_a(12, 2)
+                load_a(14, 2)
+                load_d(3)
             add_and_store(i, acc)
             previous[0] = ("last add", u) if t == PACK - 1 else None
             if t == PACK - 1:

@@ -30,10 +30,9 @@ OPENING = 2 * PACK
 LEAD = 2
 RUN_EVERY = 5
 SORT_FROM = 5
-ED_AHEAD = 3
+ED_AHEAD = 2
 BACKLOG = 3
-SHARE = 5
-SHARE_LAST = 3
+SHARE = 3
 PAUSE = 4
 
 
@@ -84,7 +83,7 @@ def tile_sector_emission_changes_g6_kernel(tc, x_words, x_scales, a, d, e, out_0
 
         def load_x(h, kg0, kg1):
             x_sb = keep.tile([P, kg1 - kg0, BANK], I32, name="x_%d_%d" % (h, kg0), align_bytes=64)
-            src = x_words[kg0:kg1, :, h * BANK:(h + 1) * BANK, :].rearrange("g p n t -> p g (n t)")
+            src = x_words[kg0:kg1, :, h * BANK:(h + 1) * BANK, :].rearrange("kg p c r -> p kg (c r)")
             nc.sync.dma_start(out=x_sb[:], in_=src.bitcast(I32))
             for kg in range(kg0, kg1):
                 x_codes[(kg, h)] = x_sb[:, kg - kg0, :]
@@ -108,8 +107,8 @@ def tile_sector_emission_changes_g6_kernel(tc, x_words, x_scales, a, d, e, out_0
         load_x(0, 0, 2)
         load_x(0, 2, 4)
         load_a(3, 1)
-        load_a(4, 1)
         load_d(0, 0, 1)
+        load_a(4, 1)
         load_a(5, 1)
         load_a(6, 2)
         load_d(1, 0, 1)
@@ -125,7 +124,7 @@ def tile_sector_emission_changes_g6_kernel(tc, x_words, x_scales, a, d, e, out_0
         a_plane = {}
 
         def sort_pairs(copy, j, kg0, kg1):
-            src = a_rows[j][:, kg0 * 2 * P:kg1 * 2 * P].rearrange("m (k p u) -> m k u p", p=P, u=2)
+            src = a_rows[j][:, kg0 * 2 * P:kg1 * 2 * P].rearrange("m (kg p odd) -> m kg odd p", p=P, odd=2)
             copy(out=sorted_pairs[j][:, kg0:kg1, :, :], in_=src)
 
         def transpose_tile(j):
@@ -134,23 +133,23 @@ def tile_sector_emission_changes_g6_kernel(tc, x_words, x_scales, a, d, e, out_0
                 bank = psum.tile([P, 2, 2, P], F32, name="t_bank")
                 for kk in range(2):
                     kg = 2 * half + kk
-                    for u in range(2):
-                        src = sorted_pairs[j][:, kg, u, :] if j >= SORT_FROM else a_pairs[(j, kg)][:, u::2]
-                        nc.tensor.transpose(bank[:, kk, u, :], src, ident[:])
+                    for odd in range(2):
+                        src = sorted_pairs[j][:, kg, odd, :] if j >= SORT_FROM else a_pairs[(j, kg)][:, odd::2]
+                        nc.tensor.transpose(bank[:, kk, odd, :], src, ident[:])
                 dst = grouped[:, half * 2 * K_PASS:(half + 1) * 2 * K_PASS].bitcast(F32)
-                nc.scalar.copy(out=dst.rearrange("p (k m u) -> p k m u", k=2, u=2),
-                               in_=bank[:].rearrange("p k u m -> p k m u"))
+                nc.scalar.copy(out=dst.rearrange("p (kk m odd) -> p kk m odd", kk=2, odd=2),
+                               in_=bank[:].rearrange("p kk odd m -> p kk m odd"))
             return grouped
 
         def quantize_a(j, grouped):
             a_codes[j] = work.tile([P, PASSES * P], I32, name="a_codes", bufs=10, align_bytes=64)
             a_plane[j] = work.tile([P, PASSES * P], U8, name="a_plane", bufs=10, align_bytes=64)
             pieces = 2 if j == 0 else 1
-            w = PASSES * P // pieces
+            words = PASSES * P // pieces
             for n in range(pieces):
-                nc.vector.quantize_mx(out=a_codes[j][:, n * w:(n + 1) * w].bitcast(FP8X4),
-                                      scales=a_plane[j][:, n * w:(n + 1) * w],
-                                      in_=grouped[:, n * w * PACK:(n + 1) * w * PACK])
+                nc.vector.quantize_mx(out=a_codes[j][:, n * words:(n + 1) * words].bitcast(FP8X4),
+                                      scales=a_plane[j][:, n * words:(n + 1) * words],
+                                      in_=grouped[:, n * words * PACK:(n + 1) * words * PACK])
 
         ed = []
         y = {}
@@ -196,8 +195,8 @@ def tile_sector_emission_changes_g6_kernel(tc, x_words, x_scales, a, d, e, out_0
 
         def interleave(copy, u, y_bf, lo, hi):
             g, c0, w = UNITS[u]
-            copy(out=y_bf[:, lo * PACK:hi * PACK].rearrange("p (c i t) -> p c t i", i=4, t=PACK),
-                 in_=y[g][:, :, c0 + lo:c0 + hi].rearrange("p t (c i) -> p c t i", i=4))
+            copy(out=y_bf[:, lo * PACK:hi * PACK].rearrange("p (c near t) -> p c t near", near=4, t=PACK),
+                 in_=y[g][:, :, c0 + lo:c0 + hi].rearrange("p t (c near) -> p c t near", near=4))
 
         def quantize_y(u, y_bf):
             g, c0, w = UNITS[u]
@@ -207,7 +206,7 @@ def tile_sector_emission_changes_g6_kernel(tc, x_words, x_scales, a, d, e, out_0
                                   in_=y_bf[:])
             lo = c0 if g == PASSES - 1 else 0
             if g == PASSES - 1 or c0 > 0:
-                dst = out_1[g, :, lo:c0 + w, :].rearrange("p n t -> p (n t)")
+                dst = out_1[g, :, lo:c0 + w, :].rearrange("p c t -> p (c t)")
                 nc.sync.dma_start(out=dst.bitcast(I32), in_=y_codes[g][:, lo:c0 + w])
 
         vector_tasks = []
@@ -234,14 +233,15 @@ def tile_sector_emission_changes_g6_kernel(tc, x_words, x_scales, a, d, e, out_0
             y_bf = work.tile([P, w * PACK], BF16, name="y_bf", bufs=2, align_bytes=64)
             is_last = u == len(UNITS) - 1
             shared = PACK * (u + 1) >= last_run_at
-            mine = w - (SHARE_LAST if is_last else SHARE) * w // 8 if shared else w
+            mine = w - SHARE * w // 8 if shared else w
             if PACK * (u + 1) == last_run_at:
                 scalar_tasks.append(lambda: interleave(nc.scalar.copy, u, y_bf, mine, w))
             elif shared:
                 interleave(nc.scalar.copy, u, y_bf, mine, w)
             cuts = [0, mine] if shared else [0, w // 2, w]
             for lo, hi in zip(cuts, cuts[1:]):
-                vector_tasks.append(("interleave", u, lambda lo=lo, hi=hi: interleave(nc.vector.tensor_copy, u, y_bf, lo, hi)))
+                vector_tasks.append(("interleave", u,
+                                     lambda lo=lo, hi=hi: interleave(nc.vector.tensor_copy, u, y_bf, lo, hi)))
             if shared and not is_last:
                 vector_tasks.extend([("pause", u, None)] * PAUSE)
             vector_tasks.append(("quantize y", u, lambda: quantize_y(u, y_bf)))
@@ -253,15 +253,16 @@ def tile_sector_emission_changes_g6_kernel(tc, x_words, x_scales, a, d, e, out_0
                 scalar_tasks.append(lambda: sort_pairs(nc.scalar.copy, j, mine, PASSES))
             return ("sort", j, lambda: sort_pairs(nc.vector.tensor_copy, j, 0, mine))
 
-        def do_run(r):
-            tiles = runs[r][1]
+        def do_run(run):
+            tiles = runs[run][1]
             staged = [transpose_tile(j) for j in tiles]
             vector_turn()
             quantize_a(tiles[0], staged[0])
             previous[0] = None
-            urgent = [("quantize a", j, lambda j=j, src=src: quantize_a(j, src)) for j, src in zip(tiles[1:], staged[1:])]
-            for later in range(r + 1, len(runs)):
-                if later - r == (2 if len(runs[later][1]) == 1 else 1):
+            urgent = [("quantize a", j, lambda j=j, src=src: quantize_a(j, src))
+                      for j, src in zip(tiles[1:], staged[1:])]
+            for later in range(run + 1, len(runs)):
+                if later - run == (2 if len(runs[later][1]) == 1 else 1):
                     urgent.extend([plan_sort(j) for j in runs[later][1] if j >= SORT_FROM])
             for n, task in enumerate(urgent):
                 vector_tasks.insert(n, task)

from contextlib import ExitStack

import concourse.mybir as mybir
from concourse.masks import make_identity

S, M = 2048, 1024
FLOPS = 2 * S * S * M

F32 = mybir.dt.float32
BF16 = mybir.dt.bfloat16
I32 = mybir.dt.int32
U8 = mybir.dt.uint8
FP8X4 = mybir.dt.float8_e4m3fn_x4
ALU = mybir.AluOpType
ACT = mybir.ActivationFunctionType

P = 128
PACK = 4
K_PASS = P * PACK
PASSES = S // K_PASS
ROW_TILES = S // P
BANK = 512
QUADRANTS = 4

UNITS = [(0, 0, BANK), (1, 0, BANK), (0, BANK, BANK), (1, BANK, BANK), (2, 0, BANK), (2, BANK, BANK), (3, 0, BANK),
         (3, BANK, BANK // 2), (3, BANK + BANK // 2, BANK // 2)]
GROUPS = [(u, t) for u in range(len(UNITS)) for t in range(PACK)]
OPENING = 2 * PACK

LEAD = 2
RUN_EVERY = 5
SORT_FROM = 5
ED_AHEAD = 2
BACKLOG = 3
SHARE = 3
PAUSE = 4


def transpose_runs():
    runs = [(max(0, j - LEAD), [j]) for j in range(OPENING)]
    last_use = GROUPS.index((UNITS.index((PASSES - 1, 0, BANK)), 2))
    doubles = list(range(OPENING, ROW_TILES, 2))
    for n, j in enumerate(doubles):
        runs.append((last_use - LEAD - RUN_EVERY * (len(doubles) - 1 - n), [j, j + 1]))
    return runs


def tile_sector_emission_changes_g6_kernel(tc, x_words, x_scales, a, d, e, out_0, out_1, out_2):
    nc = tc.nc
    runs = transpose_runs()
    last_run_at = runs[-1][0]

    with ExitStack() as ctx:
        keep = ctx.enter_context(tc.tile_pool(name="keep", bufs=1))
        work = ctx.enter_context(tc.tile_pool(name="work", bufs=2))
        psum = ctx.enter_context(tc.psum_pool(name="psum", bufs=4))
        ctx.enter_context(tc.manual_schedule())

        x_plane = keep.tile([P, M], U8, name="x_plane", align_bytes=64)
        nc.gpsimd.memset(x_plane[:].bitcast(I32), 0)
        ident = keep.tile([P, P], F32, name="ident")
        make_identity(nc, ident[:])
        y_plane = keep.tile([P, M], U8, name="y_plane", align_bytes=64)
        e_bf = keep.tile([P, PASSES, PACK], BF16, name="e_bf")
        e_f32 = keep.tile([P, PASSES, PACK], F32, name="e_f32")

        a_pairs = {}
        a_rows = {}
        x_codes = {}
        d_rows = {}

        def load_a(j0, count, kg0=0, kg1=PASSES):
            g, t0 = divmod(j0, PACK)
            tag = "a_double" if count == 2 else "a_%d_%d" % (j0, kg0)
            a_sb = keep.tile([P, count, (kg1 - kg0) * K_PASS], BF16, name=tag, bufs=3 if count == 2 else 1,
                             align_bytes=64)
            rows = a[g * K_PASS:(g + 1) * K_PASS, kg0 * K_PASS:kg1 * K_PASS].rearrange("(m t) k -> m t k", t=PACK)
            nc.sync.dma_start(out=a_sb[:], in_=rows[:, t0:t0 + count, :])
            for n in range(count):
                a_rows[j0 + n] = a_sb[:, n, :].bitcast(F32)
                for kg in range(kg0, kg1):
                    a_pairs[(j0 + n, kg)] = a_rows[j0 + n][:, (kg - kg0) * 2 * P:(kg - kg0 + 1) * 2 * P]

        def load_x(h, kg0, kg1):
            x_sb = keep.tile([P, kg1 - kg0, BANK], I32, name="x_%d_%d" % (h, kg0), align_bytes=64)
            src = x_words[kg0:kg1, :, h * BANK:(h + 1) * BANK, :].rearrange("kg p c r -> p kg (c r)")
            nc.sync.dma_start(out=x_sb[:], in_=src.bitcast(I32))
            for kg in range(kg0, kg1):
                x_codes[(kg, h)] = x_sb[:, kg - kg0, :]

        def load_d(g, h0=0, h1=2):
            d_sb = keep.tile([P, PACK, (h1 - h0) * BANK], BF16, name="d_%d_%d" % (g, h0))
            src = d[g * K_PASS:(g + 1) * K_PASS, h0 * BANK:h1 * BANK].rearrange("(p t) c -> p t c", t=PACK)
            nc.sync.dma_start(out=d_sb[:], in_=src)
            for h in range(h0, h1):
                d_rows[(g, h)] = d_sb[:, :, (h - h0) * BANK:(h - h0 + 1) * BANK]

        load_a(0, 1, 0, 2)
        nc.scalar.dma_start(out=e_bf[:], in_=e.rearrange("(g p t) -> p g t", p=P, t=PACK))
        load_a(0, 1, 2, 4)
        load_a(1, 1)
        for q in range(QUADRANTS):
            nc.scalar.dma_start(out=x_plane[32 * q:32 * q + 16, :].bitcast(I32),
                                in_=x_scales[:, 4 * q:4 * q + 4, :].bitcast(I32))
        nc.scalar.activation(out=e_f32[:], in_=e_bf[:], func=ACT.Copy)
        load_a(2, 1)
        load_x(0, 0, 2)
        load_x(0, 2, 4)
        load_a(3, 1)
        load_d(0, 0, 1)
        load_a(4, 1)
        load_a(5, 1)
        load_a(6, 2)
        load_d(1, 0, 1)
        load_x(1, 0, 4)
        load_a(8, 2)
        load_d(0, 1, 2)
        load_d(1, 1, 2)
        load_a(10, 2)
        load_d(2)

        sorted_pairs = {}
        a_codes = {}
        a_plane = {}

        def sort_pairs(copy, j, kg0, kg1):
            src = a_rows[j][:, kg0 * 2 * P:kg1 * 2 * P].rearrange("m (kg p odd) -> m kg odd p", p=P, odd=2)
            copy(out=sorted_pairs[j][:, kg0:kg1, :, :], in_=src)

        def transpose_tile(j):
            grouped = work.tile([P, PASSES * K_PASS], BF16, name="grouped", bufs=4, align_bytes=64)
            for half in range(2):
                bank = psum.tile([P, 2, 2, P], F32, name="t_bank")
                for kk in range(2):
                    kg = 2 * half + kk
                    for odd in range(2):
                        src = sorted_pairs[j][:, kg, odd, :] if j >= SORT_FROM else a_pairs[(j, kg)][:, odd::2]
                        nc.tensor.transpose(bank[:, kk, odd, :], src, ident[:])
                dst = grouped[:, half * 2 * K_PASS:(half + 1) * 2 * K_PASS].bitcast(F32)
                nc.scalar.copy(out=dst.rearrange("p (kk m odd) -> p kk m odd", kk=2, odd=2),
                               in_=bank[:].rearrange("p kk odd m -> p kk m odd"))
            return grouped

        def quantize_a(j, grouped):
            a_codes[j] = work.tile([P, PASSES * P], I32, name="a_codes", bufs=10, align_bytes=64)
            a_plane[j] = work.tile([P, PASSES * P], U8, name="a_plane", bufs=10, align_bytes=64)
            pieces = 2 if j == 0 else 1
            words = PASSES * P // pieces
            for n in range(pieces):
                nc.vector.quantize_mx(out=a_codes[j][:, n * words:(n + 1) * words].bitcast(FP8X4),
                                      scales=a_plane[j][:, n * words:(n + 1) * words],
                                      in_=grouped[:, n * words * PACK:(n + 1) * words * PACK])

        ed = []
        y = {}
        y_codes = {}

        def scale_d():
            u, t = GROUPS[len(ed)]
            g, c0, w = UNITS[u]
            h, off = divmod(c0, BANK)
            ed_sb = work.tile([P, w], F32, name="ed_%d" % w, bufs=ED_AHEAD + 2 if w == BANK else 2 * PACK)
            nc.scalar.activation(out=ed_sb[:], in_=d_rows[(g, h)][:, t, off:off + w], func=ACT.Copy,
                                 scale=e_f32[:, g, t:t + 1])
            ed.append(ed_sb)

        def multiply(i):
            u, t = GROUPS[i]
            g, c0, w = UNITS[u]
            h, off = divmod(c0, BANK)
            j = PACK * g + t
            spare = i >= len(GROUPS) - 2 * PACK - 1 and i % 2 == 1
            acc = psum.tile([P, w], F32, name="acc", tag="t_bank" if spare else "acc")
            for kg in range(PASSES):
                nc.tensor.matmul_mx(
                    out=acc[:],
                    lhsT=a_codes[j][:, kg * P:(kg + 1) * P].bitcast(FP8X4),
                    lhsT_scale=a_plane[j][:, kg * P:(kg + 1) * P],
                    rhs=x_codes[(kg, h)][:, off:off + w].bitcast(FP8X4),
                    rhs_scale=x_plane[4 * kg:P, c0:c0 + w],
                    start=(kg == 0), stop=(kg == PASSES - 1))
            return acc

        def add_and_store(i, acc):
            u, t = GROUPS[i]
            g, c0, w = UNITS[u]
            if g not in y:
                y[g] = work.tile([P, PACK, M], F32, name="y", bufs=3, align_bytes=64)
            nc.vector.scalar_tensor_tensor(out=y[g][:, t, c0:c0 + w], in0=acc[:], scalar=e_f32[:, g, t:t + 1],
                                           in1=ed[i][:], op0=ALU.mult, op1=ALU.add)
            lo = c0 if g == PASSES - 1 else 0
            if t % 2 == 1 and (g == PASSES - 1 or c0 > 0):
                dst = out_0[g * K_PASS:(g + 1) * K_PASS, :].rearrange("(p t) c -> p t c", t=PACK)
                nc.sync.dma_start(out=dst[:, t - 1:t + 1, lo:c0 + w], in_=y[g][:, t - 1:t + 1, lo:c0 + w])

        def interleave(copy, u, y_bf, lo, hi):
            g, c0, w = UNITS[u]
            copy(out=y_bf[:, lo * PACK:hi * PACK].rearrange("p (c near t) -> p c t near", near=4, t=PACK),
                 in_=y[g][:, :, c0 + lo:c0 + hi].rearrange("p t (c near) -> p c t near", near=4))

        def quantize_y(u, y_bf):
            g, c0, w = UNITS[u]
            if g not in y_codes:
                y_codes[g] = work.tile([P, M], I32, name="y_codes", bufs=2, align_bytes=64)
            nc.vector.quantize_mx(out=y_codes[g][:, c0:c0 + w].bitcast(FP8X4), scales=y_plane[4 * g:P, c0:c0 + w],
                                  in_=y_bf[:])
            lo = c0 if g == PASSES - 1 else 0
            if g == PASSES - 1 or c0 > 0:
                dst = out_1[g, :, lo:c0 + w, :].rearrange("p c t -> p (c t)")
                nc.sync.dma_start(out=dst.bitcast(I32), in_=y_codes[g][:, lo:c0 + w])

        vector_tasks = []
        scalar_tasks = []
        previous = [None]

        def vector_turn():
            for n, (kind, key, call) in enumerate(vector_tasks):
                earlier = [(k, other) for k, other, unused in vector_tasks[:n]]
                if kind == "interleave" and previous[0] == ("last add", key):
                    continue
                if kind == "quantize y" and previous[0] == ("interleave", key):
                    continue
                if kind in ("pause", "quantize y") and (("interleave", key) in earlier or ("pause", key) in earlier):
                    continue
                vector_tasks.pop(n)
                if kind != "pause":
                    call()
                    previous[0] = (kind, key)
                return

        def plan_planes(u):
            w = UNITS[u][2]
            y_bf = work.tile([P, w * PACK], BF16, name="y_bf", bufs=2, align_bytes=64)
            is_last = u == len(UNITS) - 1
            shared = PACK * (u + 1) >= last_run_at
            mine = w - SHARE * w // 8 if shared else w
            if PACK * (u + 1) == last_run_at:
                scalar_tasks.append(lambda: interleave(nc.scalar.copy, u, y_bf, mine, w))
            elif shared:
                interleave(nc.scalar.copy, u, y_bf, mine, w)
            cuts = [0, mine] if shared else [0, w // 2, w]
            for lo, hi in zip(cuts, cuts[1:]):
                vector_tasks.append(("interleave", u,
                                     lambda lo=lo, hi=hi: interleave(nc.vector.tensor_copy, u, y_bf, lo, hi)))
            if shared and not is_last:
                vector_tasks.extend([("pause", u, None)] * PAUSE)
            vector_tasks.append(("quantize y", u, lambda: quantize_y(u, y_bf)))

        def plan_sort(j):
            sorted_pairs[j] = work.tile([P, PASSES, 2, P], F32, name="sorted", bufs=3, align_bytes=64)
            mine = PASSES if j < OPENING else PASSES // 2
            if mine < PASSES:
                scalar_tasks.append(lambda: sort_pairs(nc.scalar.copy, j, mine, PASSES))
            return ("sort", j, lambda: sort_pairs(nc.vector.tensor_copy, j, 0, mine))

        def do_run(run):
            tiles = runs[run][1]
            staged = [transpose_tile(j) for j in tiles]
            vector_turn()
            quantize_a(tiles[0], staged[0])
            previous[0] = None
            urgent = [("quantize a", j, lambda j=j, src=src: quantize_a(j, src))
                      for j, src in zip(tiles[1:], staged[1:])]
            for later in range(run + 1, len(runs)):
                if later - run == (2 if len(runs[later][1]) == 1 else 1):
                    urgent.extend([plan_sort(j) for j in runs[later][1] if j >= SORT_FROM])
            for n, task in enumerate(urgent):
                vector_tasks.insert(n, task)

        def epilogue(i, acc):
            u, t = GROUPS[i]
            while len(ed) <= i:
                scale_d()
            if i >= OPENING:
                target = i + 1 + ED_AHEAD if i < last_run_at else len(GROUPS)
                for n in range(min(2, target - len(ed))):
                    scale_d()
            if scalar_tasks:
                scalar_tasks.pop(0)()
            if i == OPENING:
                load_a(12, 2)
                load_a(14, 2)
                load_d(3)
            add_and_store(i, acc)
            previous[0] = ("last add", u) if t == PACK - 1 else None
            if t == PACK - 1:
                plan_planes(u)
            vector_turn()
            if i >= OPENING and len(vector_tasks) >= BACKLOG:
                vector_turn()

        next_run = 0
        first = None
        for i in range(len(GROUPS)):
            while next_run < len(runs) and runs[next_run][0] <= i:
                do_run(next_run)
                next_run = next_run + 1
            if i == 1:
                epilogue(0, first)
            acc = multiply(i)
            if i == 0:
                first = acc
            else:
                epilogue(i, acc)
        while vector_tasks:
            vector_turn()
            previous[0] = None
        for q in range(QUADRANTS):
            queue = nc.scalar if q % 2 else nc.sync
            queue.dma_start(out=out_2[:, 4 * q:4 * q + 4, :].bitcast(I32),
                            in_=y_plane[32 * q:32 * q + 16, :].bitcast(I32))
